import numpy as np, ml_dtypes
CORES = [78,86,94,102,110,118]
N = 6
import mx_ref
BF = ml_dtypes.bfloat16
def entries(a):
    return np.ascontiguousarray(a.T).reshape(-1)
def table(e):
    return np.ascontiguousarray(np.reshape(e, (-1, 16)).T).astype(np.int32)
def cut(t, i, w=512):
    return t[:, w * i:w * i + w]
def f(rng, *shape):
    return mx_ref.flush((rng.standard_normal(shape, dtype=np.float32) * np.exp2(rng.integers(-2, 3, shape[:-1] + (1,)))).astype(BF))
def wide(rng, *shape, cols=0):
    v = rng.standard_normal(shape, dtype=np.float32) * np.exp2(rng.integers(-12, 13, shape)).astype(np.float32)
    if cols: v *= np.repeat(np.exp2(rng.integers(-cols, cols + 1, shape[:-2] + (1, shape[-1] // 4))) * (rng.random(shape[:-2] + (1, shape[-1] // 4)) > 0.0625), 4, axis=-1).astype(np.float32)
    return mx_ref.flush(v.astype(BF))
SH, CH, R = 192, 32, 3
def lists(rng, how=""):
    o = []
    for q in range(N):
        p = rng.permutation(SH); h = int(rng.integers(0, 2)); e = []
        for t in range(R):
            if how == "same": v = p[:CH]
            elif how == "apart": v = p[CH * t:CH * t + CH]
            elif how == "ends": v = np.arange(CH) + (SH - CH) * ((h + t) % 2)
            elif how == "pairs": v = p[CH:2 * CH] if t >= 2 - h else p[:CH]
            else: v = rng.permutation(SH)[:CH]
            e.append(rng.permutation(v))
        o.append(table(np.concatenate(e)))
    return np.stack(o)
def fit(v):
    v = np.array(v); v[np.abs(v.astype(np.float32)) < np.float32(2.0 ** -30)] = 0
    return v
def setup_inputs(rng):
    return {"x": f(rng, N, 128, 512 * (R + 1)), "wm": f(rng, N, 128, 4 * SH), "dl": f(rng, N, 128, 4 * R * CH), "ix": lists(rng)}
def setup_inputs_same(rng):
    d = setup_inputs(rng); d["ix"] = lists(rng, "same"); return d
def setup_inputs_apart(rng):
    d = setup_inputs(rng); d["ix"] = lists(rng, "apart"); return d
def setup_inputs_ends(rng):
    d = setup_inputs(rng); d["ix"] = lists(rng, "ends"); return d
def setup_inputs_pairs(rng):
    d = setup_inputs(rng); d["ix"] = lists(rng, "pairs"); return d
def setup_inputs_spread(rng):
    d = setup_inputs(rng); d["wm"] = fit(wide(rng, N, 128, 4 * SH, cols=6)); d["dl"] = fit(wide(rng, N, 128, 4 * R * CH, cols=6)); return d
def check_inputs(d):
    b = []
    for n in ("x", "wm", "dl"):
        v = np.abs(np.asarray(d[n]).astype(np.float32))
        if not np.isfinite(v).all() or ((v > 0) & ((v < 2.0 ** -30) | (v > 2.0 ** 30))).any(): b.append(n)
    for q in range(N):
        e = entries(d["ix"][q])
        if e.min() < 0 or e.max() >= SH or any(len(set(e[CH * t:CH * t + CH].tolist())) != CH for t in range(R)): b.append("ix")
    return b
def reference(x, wm, dl, ix):
    X = [[mx_ref.quantize(np.ascontiguousarray(cut(x[r], t))) for t in range(R + 1)] for r in range(N)]
    y = np.zeros((N, 128, (R + 1) * N * SH), np.float32)
    for q in range(N):
        W = np.array(wm[q]).reshape(128, SH, 4); new = np.array(dl[q]).reshape(128, R * CH, 4); e = entries(ix[q])
        for t in range(R + 1):
            if t: W[:, e[CH * (t - 1):CH * t]] = new[:, CH * (t - 1):CH * t]
            held = mx_ref.quantize(np.array(W).reshape(128, 4 * SH)); k = SH * (t * N + q)
            for r in range(N): y[r][:, k:k + SH] = mx_ref.matmul(X[r][t], held)
    return {"y": y}

@@ -1,0 +1,323 @@
+from concourse.bass import DstId, RemoteDMATransfer
+from concourse.mybir import dt, AluOpType, ActivationFunctionType
+
+N, SH, CH, R = 6, 192, 32, 3
+ND = R * CH
+NP = ND + SH
+TC = SH // 16
+LC = R * TC
+SLOTS = range(1, N)
+VIA_A, VIA_B = (2, 4), (3, 5)
+
+SCRATCH = {
+    "wt": ("sbuf", [128, 4 * NP], "bfloat16"),
+    "xs": ("sbuf", [128, 512 * (R + 1)], "bfloat16"),
+    "xq": ("sbuf", [128, 128 * (R + 1)], "float8_e4m3fn_x4"),
+    "xqs": ("sbuf", [128, 128 * (R + 1)], "uint8"),
+    "pool": ("sbuf", [128, NP], "float8_e4m3fn_x4"),
+    "pools": ("sbuf", [128, NP], "uint8"),
+    "hop": ("sbuf", [128, NP], "float8_e4m3fn_x4"),
+    "hops": ("sbuf", [128, NP], "uint8"),
+    "ixa": ("sbuf", [128, ND], "int32"),
+    "ixr": ("sbuf", [128, ND], "int32"),
+    "ixb": ("sbuf", [128, ND], "bfloat16"),
+    "stepc": ("sbuf", [128, ND], "bfloat16"),
+    "pnum": ("sbuf", [128, TC], "int32"),
+    "plow": ("sbuf", [128, TC], "int32"),
+    "mnum": ("sbuf", [128, TC], "int32"),
+    "ccol": ("sbuf", [128, TC], "float32"),
+    "first": ("sbuf", [128, TC], "float32"),
+    "ne": ("sbuf", [128, TC * ND], "bfloat16"),
+    "stt": ("sbuf", [128, TC * ND], "bfloat16"),
+    "tab": ("sbuf", [128, LC], "uint16"),
+    "tabd": ("dram", [128, LC // 4], "uint16"),
+    "ys": ("sbuf", [128, (R + 1) * N * SH], "float32"),
+    "acc": ("psum", [128, 8 * 512], "float32"),
+}
+for _s in range(N):
+    SCRATCH["pk%d" % _s] = ("sbuf", [128, R * SH], "float8_e4m3fn_x4")
+    SCRATCH["pks%d" % _s] = ("sbuf", [128, R * SH], "uint8")
+for _s in SLOTS:
+    SCRATCH["land%d" % _s] = ("sbuf", [128, NP], "float8_e4m3fn_x4")
+    SCRATCH["lands%d" % _s] = ("sbuf", [128, NP], "uint8")
+    SCRATCH["off%d" % _s] = ("sbuf", [128, LC], "uint16")
+    if _s > 1:
+        SCRATCH["lst%d" % _s] = ("dram", [128, LC // 4], "uint16")
+
+SEMAPHORES = (["ldw", "ldi", "pb", "num", "vc", "qd", "tab", "tabd", "xl0", "xl1", "xq0", "xq1", "sent", "st", "hc", "hs"]
+              + ["ar%d" % s for s in SLOTS] + ["ls%d" % s for s in SLOTS] + ["rp%d" % s for s in SLOTS if s > 1]
+              + ["%s%d%d" % (k, s, t) for k in ("pv", "ps") for s in range(N) for t in (1, 2, 3)]
+              + ["%s%d%d" % (k, s, t) for k in ("mm", "ev") for s in range(N) for t in range(R + 1)])
+
+
+def source(r, s):
+    a, e = r // 2, r % 2
+    return 2 * ((a + s // 2) % (N // 2)) + (e if s % 2 == 0 else 1 - e)
+
+
+def dest(q, s):
+    return [r for r in range(N) if source(r, s) == q][0]
+
+
+def bits(engines):
+    m = 0
+    for e in engines:
+        m |= 1 << e
+    return m
+
+
+def relays(core, cores, topo):
+    q = cores.index(core)
+    mine = [c for c in topo.cores_of(core) if c != core]
+
+    def fit(same, slots):
+        return [c for c in mine if (topo.die(c) == topo.die(core)) == same
+                and all(topo.may_write(c, cores[dest(q, s)]) for s in slots)][0]
+    return fit(False, VIA_A), fit(True, VIA_B)
+
+
+def relay_engines(core, relay, cores, topo):
+    off = topo.engines(core, cores[dest(cores.index(core), 1)])
+    return [e for e in topo.engines(core, relay) if e not in off]
+
+
+def rank_program(g, core, T, topo):
+    cores = list(T.cores)
+    rank = T.rank_of(core)
+
+    def at(c):
+        a = topo.addr(c)
+        return DstId(rid=a[0], pnc=a[1])
+
+    def send(src, dst, sem, to, engines):
+        a = topo.addr(to)
+        g.remote_dma(dst, src, sem, T.sem.sent, a[1], a[0], bits(engines))
+        return len(engines)
+
+    if rank is None:
+        for q, c in enumerate(cores):
+            if core not in topo.cores_of(c):
+                continue
+            a, b = relays(c, cores, topo)
+            slots = VIA_A if core == a else VIA_B if core == b else ()
+            full = len(relay_engines(c, core, cores, topo))
+            n = 0
+            for s in slots:
+                to = cores[dest(q, s)]
+                eng = topo.engines(core, to)
+                if s == slots[0]:
+                    g.wait_ge(T.sem.hs, full // 2)
+                n += send(T.hops[:], T["lands%d" % s][:], T.sem["ar%d" % s], to, eng)
+                if s == slots[0]:
+                    g.wait_ge(T.sem.hc, full)
+                n += send(T.hop[:].bitcast(dt.uint8), T["land%d" % s][:].bitcast(dt.uint8), T.sem["ar%d" % s], to, eng)
+            if n:
+                g.wait_ge(T.sem.sent, n)
+        return
+
+    V, S, P, Y = g.vector, g.scalar, g.tensor, g.sync
+    relay_a, relay_b = relays(core, cores, topo)
+    far = [None] + [cores[dest(rank, s)] for s in SLOTS]
+    off_eng = topo.engines(core, far[1])
+
+    Y.dma_start(T.wt[:, 4 * ND:4 * NP], T.wm[:]).then_inc(T.sem.ldw, 16)
+    for t in range(R):
+        S.dma_start(T.ixa[0:1, CH * t:CH * t + CH], T.ix[:, 2 * t:2 * t + 2]).then_inc(T.sem.ldi, 16)
+    S.dma_start(T.wt[:, 0:4 * ND], T.dl[:]).then_inc(T.sem.ldw, 16)
+    h = 256 * (R + 1)
+    for i in range(2):
+        S.dma_start(T.xs[:, h * i:h * i + h], T.x[:, h * i:h * i + h]).then_inc(T.sem["xl%d" % i], 16)
+
+    g.iota(T.pnum[:], [[0, TC]], 0, 1).then_inc(T.sem.num, 1)
+    g.iota(T.mnum[:], [[16, TC]], 0, 0).then_inc(T.sem.num, 1)
+    g.wait_ge(T.sem.ldi, 16 * R)
+    g.partition_broadcast(T.ixr[:], T.ixa[0:1, :], 128).then_inc(T.sem.pb, 1)
+
+    def pools(scale, slots, to):
+        src = T.pools[:] if scale else T.pool[:].bitcast(dt.uint8)
+        tr = []
+        for s in slots:
+            land = T["lands%d" % s][:] if scale else T["land%d" % s][:].bitcast(dt.uint8)
+            tr.append((far[s], topo.engines(core, far[s]), T.sem["ar%d" % s], land))
+        for i, relay in enumerate(to):
+            e = relay_engines(core, relay, cores, topo)
+            w = len(e) // len(to)
+            tr.append((relay, e[w * i:w * i + w], T.sem.hs if scale else T.sem.hc,
+                       T.hops[:] if scale else T.hop[:].bitcast(dt.uint8)))
+        g.remote_dma_fused([RemoteDMATransfer(dst_ids=[at(c)], dma_engine_mask=bits(e), remote_sem=m, srcs=[src], dsts=[d])
+                            for c, e, m, d in tr], local_sem=T.sem.sent)
+        return sum(len(e) for c, e, m, d in tr)
+
+    share = len(off_eng) // (N - 2)
+
+    def lists():
+        tr = []
+        for i, s in enumerate(range(2, N)):
+            e = topo.engines(core, far[s])[share * i:share * i + share]
+            tr.append(RemoteDMATransfer(dst_ids=[at(far[s])], dma_engine_mask=bits(e), remote_sem=T.sem["ls%d" % s],
+                                        srcs=[T.tabd[:]], dsts=[T["lst%d" % s][:]]))
+        g.remote_dma_fused(tr, local_sem=T.sem.sent)
+        return share * (N - 2)
+
+    g.wait_ge(T.sem.qd, 1)
+    sent = pools(True, (1,), (relay_a, relay_b))
+    sent += pools(False, (1,), (relay_a,))
+    g.wait_ge(T.sem.tab, R)
+    sent += send(T.tab[:], T.off1[:], T.sem.ls1, far[1], off_eng)
+    sent += pools(False, (), (relay_b,))
+    g.wait_ge(T.sem.tabd, 16)
+    sent += lists()
+    g.wait_ge(T.sem.sent, sent)
+
+    vc = [0]
+
+    def v(ins):
+        vc[0] += 1
+        ins.then_inc(T.sem.vc, 1)
+
+    def vwait():
+        V.wait_ge(T.sem.vc, vc[0])
+
+    v(V.memset(T.stepc[:, 0:ND:2], 16.0))
+    for t in range(R):
+        v(V.memset(T.stepc[:, CH * t + 1:CH * t + CH - 1:2], -15.0))
+    v(V.memset(T.stepc[:, CH - 1:ND:CH], 1.0))
+    V.wait_ge(T.sem.num, 2)
+    v(V.tensor_scalar(T.plow[:], T.pnum[:], 15, None, AluOpType.bitwise_and))
+    vwait()
+    v(V.tensor_tensor(T.ccol[:], T.plow[:], T.mnum[:], AluOpType.add))
+    vwait()
+    v(V.tensor_scalar(T.first[:], T.ccol[:], -1.0, float(-ND), AluOpType.mult, AluOpType.add))
+
+    V.wait_ge(T.sem.ldw, 32)
+    V.quantize_mx(T.pool[:], T.pools[:], T.wt[:]).then_inc(T.sem.qd, 1)
+
+    V.wait_ge(T.sem.pb, 1)
+    v(V.tensor_copy(T.ixb[:], T.ixr[:]))
+    vwait()
+    for m in range(TC):
+        v(V.tensor_scalar(T.ne[:, ND * m:ND * m + ND], T.ixb[:], T.ccol[:, m:m + 1], None, AluOpType.not_equal))
+    vwait()
+    for m in range(TC):
+        k = slice(ND * m, ND * m + ND)
+        v(V.tensor_tensor_scan(T.stt[:, k], T.ne[:, k], T.stepc[:], T.first[:, m:m + 1], AluOpType.mult, AluOpType.add))
+    vwait()
+    for t in range(1, R + 1):
+        V.tensor_scalar(T.tab[:, TC * (t - 1):TC * t], T.stt[:, CH * t - 1:TC * ND:ND], -1.0, float(CH * t),
+                        AluOpType.mult, AluOpType.add).then_inc(T.sem.tab, 1)
+
+    for i in range(2):
+        V.wait_ge(T.sem["xl%d" % i], 16)
+        k = slice(128 * (R + 1) // 2 * i, 128 * (R + 1) // 2 * (i + 1))
+        V.quantize_mx(T.xq[:, k], T.xqs[:, k], T.xs[:, h * i:h * i + h]).then_inc(T.sem["xq%d" % i], 1)
+
+    codes = [T.pool] + [T["land%d" % s] for s in SLOTS]
+    scales = [T.pools] + [T["lands%d" % s] for s in SLOTS]
+    offs = [T.tab] + [T["off%d" % s] for s in SLOTS]
+    eng = len(off_eng)
+
+    def have(q, s):
+        if s == 0:
+            q.wait_ge(T.sem.qd, 1)
+        else:
+            q.wait_ge(T.sem["ar%d" % s], 2 * eng)
+
+    def listed(q, s):
+        if s == 0:
+            q.wait_ge(T.sem.tab, R)
+        elif s == 1:
+            q.wait_ge(T.sem.ls1, eng)
+        else:
+            q.wait_ge(T.sem["rp%d" % s], 64)
+
+    def column(s, t):
+        return (t * N + source(rank, s)) * SH
+
+    first_t = {}
+
+    def pick(q, s, a, b):
+        have(q, s)
+        listed(q, s)
+        o = offs[s][:, TC * (a - 1):TC * b]
+        k = slice(SH * (a - 1), SH * b)
+        for t in range(a, b + 1):
+            first_t[(s, t)] = a
+        if q is V:
+            V.tensor_copy(T["pk%d" % s][:, k].bitcast(dt.uint32), codes[s][:].bitcast(dt.uint32).indirect(o)
+                          ).then_inc(T.sem["pv%d%d" % (s, a)], 1)
+        else:
+            S.activation(T["pks%d" % s][:, k], scales[s][:].indirect(o), ActivationFunctionType.Copy
+                         ).then_inc(T.sem["ps%d%d" % (s, a)], 1)
+
+    items = [(s, t) for s in range(N - 2) for t in range(R + 1)] + [(s, t) for t in range(R + 1) for s in (N - 2, N - 1)]
+
+    def bank(s, t):
+        b = 512 * (items.index((s, t)) % 8)
+        return T.acc[:, b:b + SH]
+
+    def evac(q, s, t):
+        q.wait_ge(T.sem["mm%d%d" % (s, t)], 1)
+        c = column(s, t)
+        if q is V:
+            V.tensor_copy(T.ys[:, c:c + SH], bank(s, t)).then_inc(T.sem["ev%d%d" % (s, t)], 1)
+        else:
+            S.activation(T.ys[:, c:c + SH], bank(s, t), ActivationFunctionType.Copy).then_inc(T.sem["ev%d%d" % (s, t)], 1)
+
+    for q, a, b in ((V, 0, 2), (S, 1, 3)):
+        for s in range(N - 2):
+            pick(q, s, 1, 1)
+            if s in (1, 3):
+                evac(q, s - 1, b)
+            if q is V:
+                evac(q, s, a)
+            pick(q, s, 2, 3)
+            if q is S:
+                evac(q, s, a)
+            if s == 1:
+                evac(q, s, b)
+        mine = 4 if q is V else 5
+        pick(q, 4, 1, 1)
+        evac(q, 3, b)
+        pick(q, 5, 1, 1)
+        evac(q, mine, 0)
+        for t in (2, 3):
+            pick(q, 4, t, t)
+            pick(q, 5, t, t)
+            evac(q, mine, t - 1)
+        evac(q, mine, 3)
+
+    for n, (s, t) in enumerate(items):
+        if n == 0:
+            P.wait_ge(T.sem.xq0, 1)
+        if n == 2:
+            P.wait_ge(T.sem.xq1, 1)
+        if n >= 8:
+            P.wait_ge(T.sem["ev%d%d" % items[n - 8]], 1)
+        if t == 0:
+            have(P, s)
+            rhs, rs = codes[s][:, ND:NP], scales[s][:, ND:NP]
+        else:
+            a = first_t[(s, t)]
+            if a == t:
+                P.wait_ge(T.sem["pv%d%d" % (s, a)], 1)
+                P.wait_ge(T.sem["ps%d%d" % (s, a)], 1)
+            k = slice(SH * (t - 1), SH * t)
+            rhs, rs = T["pk%d" % s][:, k], T["pks%d" % s][:, k]
+        P.matmul_mx(bank(s, t), T.xq[:, 128 * t:128 * t + 128], T.xqs[:, 128 * t:128 * t + 128], rhs, rs, True, True
+                    ).then_inc(T.sem["mm%d%d" % (s, t)], 1)
+
+    Y.wait_ge(T.sem.tab, R)
+    Y.dma_start(T.tabd[:], T.tab[0:32, :]).then_inc(T.sem.tabd, 16)
+    for s in range(2, N):
+        Y.wait_ge(T.sem["ls%d" % s], share)
+        for a in range(4):
+            Y.dma_start(T["off%d" % s][32 * a:32 * a + 32, :], T["lst%d" % s][:]).then_inc(T.sem["rp%d" % s], 16)
+    n = 0
+    for s in range(0, N, 2):
+        for t in range(R + 1):
+            c = min(column(s, t), column(s + 1, t))
+            Y.wait_ge(T.sem["ev%d%d" % (s, t)], 1)
+            Y.wait_ge(T.sem["ev%d%d" % (s + 1, t)], 1)
+            Y.dma_start(T.y[:, c:c + 2 * SH], T.ys[:, c:c + 2 * SH]).then_inc(T.sem.st, 16)
+            n += 16
+    Y.wait_ge(T.sem.st, n)

@@ -6,8 +6,12 @@ ND = R * CH
 NP = ND + SH
 TC = SH // 16
 LC = R * TC
+QD = 4
+QM = TC // QD
+QC = R * QM
 SLOTS = range(1, N)
-VIA_A, VIA_B = (2, 4), (3, 5)
+DIRECT, RELAYED = (1,), (2, 3, 4, 5)
+GROUPS = ((0,), DIRECT, RELAYED)
 
 SCRATCH = {
     "wt": ("sbuf", [128, 4 * NP], "bfloat16"),
@@ -20,43 +24,56 @@ SCRATCH = {
     "hops": ("sbuf", [128, NP], "uint8"),
     "ixa": ("sbuf", [128, ND], "int32"),
     "ixr": ("sbuf", [128, ND], "int32"),
-    "ixb": ("sbuf", [128, ND], "bfloat16"),
     "stepc": ("sbuf", [128, ND], "bfloat16"),
-    "pnum": ("sbuf", [128, TC], "int32"),
-    "plow": ("sbuf", [128, TC], "int32"),
-    "mnum": ("sbuf", [128, TC], "int32"),
-    "ccol": ("sbuf", [128, TC], "float32"),
-    "first": ("sbuf", [128, TC], "float32"),
-    "ne": ("sbuf", [128, TC * ND], "bfloat16"),
-    "stt": ("sbuf", [128, TC * ND], "bfloat16"),
-    "tab": ("sbuf", [128, LC], "uint16"),
-    "tabd": ("dram", [128, LC // 4], "uint16"),
+    "pnum": ("sbuf", [128, QM], "int32"),
+    "plow": ("sbuf", [128, QM], "int32"),
+    "prun": ("sbuf", [128, QM], "int32"),
+    "mnum": ("sbuf", [128, QM], "int32"),
+    "cpart": ("sbuf", [128, QM], "float32"),
+    "ccol": ("sbuf", [128, QM], "float32"),
+    "first": ("sbuf", [128, QM], "float32"),
+    "ne": ("sbuf", [128, QM * ND], "bfloat16"),
+    "stt": ("sbuf", [128, QM * ND], "bfloat16"),
     "ys": ("sbuf", [128, (R + 1) * N * SH], "float32"),
     "acc": ("psum", [128, 8 * 512], "float32"),
 }
+for _k, _g in enumerate(GROUPS):
+    SCRATCH["off%d" % _k] = ("sbuf", [128, LC * len(_g)], "uint16")
+    if _k != 1:
+        SCRATCH["fold%d" % _k] = ("sbuf", [128, QC * len(_g)], "uint16")
 for _s in range(N):
     SCRATCH["pk%d" % _s] = ("sbuf", [128, R * SH], "float8_e4m3fn_x4")
     SCRATCH["pks%d" % _s] = ("sbuf", [128, R * SH], "uint8")
 for _s in SLOTS:
     SCRATCH["land%d" % _s] = ("sbuf", [128, NP], "float8_e4m3fn_x4")
     SCRATCH["lands%d" % _s] = ("sbuf", [128, NP], "uint8")
-    SCRATCH["off%d" % _s] = ("sbuf", [128, LC], "uint16")
-    if _s > 1:
-        SCRATCH["lst%d" % _s] = ("dram", [128, LC // 4], "uint16")
 
-SEMAPHORES = (["ldw", "ldi", "pb", "num", "vc", "qd", "tab", "tabd", "xl0", "xl1", "xq0", "xq1", "sent", "st", "hc", "hs"]
-              + ["ar%d" % s for s in SLOTS] + ["ls%d" % s for s in SLOTS] + ["rp%d" % s for s in SLOTS if s > 1]
+SEMAPHORES = (["ldw", "ldi", "ldx", "pb", "num", "vc", "gq", "qd", "xq", "fold", "sent", "st", "hc", "hs"]
+              + ["of%d" % k for k in range(len(GROUPS))]
+              + ["%s%d" % (k, q) for k in ("ac", "as", "al") for q in range(N)]
               + ["%s%d%d" % (k, s, t) for k in ("pv", "ps") for s in range(N) for t in (1, 2, 3)]
               + ["%s%d%d" % (k, s, t) for k in ("mm", "ev") for s in range(N) for t in range(R + 1)])
 
+VECTOR = ("p013 x e02 p113 u e13 p213 p313 e21 e23 p411 e31 p511 e33 p422 e40 p522 e41 p433 p533 e42 e43").split()
+SCALAR = ("p013 e00 e01 e03 e10 p113 e11 e12 p213 e20 p313 e22 e30 p411 e32 p511 p422 e50 p522 e51 p433 p533 e52 e53").split()
+TENSOR = [(s, t) for s in range(N - 2) for t in range(R + 1)] + [(s, t) for t in range(R + 1) for s in (N - 2, N - 1)]
 
-def source(r, s):
-    a, e = r // 2, r % 2
-    return 2 * ((a + s // 2) % (N // 2)) + (e if s % 2 == 0 else 1 - e)
 
-
-def dest(q, s):
-    return [r for r in range(N) if source(r, s) == q][0]
+def sources(cores, topo):
+    chips = [topo.chip(c) for c in cores]
+    mated = [[q for q in range(N) if q != r and topo.mates(chips[r], chips[q])] for r in range(N)]
+    alone = [r for r in range(N) if not mated[r]]
+    partner = [mated[r][0] if mated[r] else [q for q in alone if q != r][0] for r in range(N)]
+    out = []
+    for r in range(N):
+        plane = [q for q in range(N) if q == r or topo.same_plane(chips[r], chips[q])]
+        i = plane.index(r)
+        row = []
+        for k in range(len(plane)):
+            q = plane[(i + k) % len(plane)]
+            row += [q, partner[q]]
+        out.append(row)
+    return out
 
 
 def bits(engines):
@@ -66,114 +83,110 @@ def bits(engines):
     return m
 
 
-def relays(core, cores, topo):
-    q = cores.index(core)
+def relays(core, far, topo):
     mine = [c for c in topo.cores_of(core) if c != core]
 
-    def fit(same, slots):
+    def fit(same):
         return [c for c in mine if (topo.die(c) == topo.die(core)) == same
-                and all(topo.may_write(c, cores[dest(q, s)]) for s in slots)][0]
-    return fit(False, VIA_A), fit(True, VIA_B)
-
-
-def relay_engines(core, relay, cores, topo):
-    off = topo.engines(core, cores[dest(cores.index(core), 1)])
-    return [e for e in topo.engines(core, relay) if e not in off]
+                and all(topo.may_write(c, far[s]) for s in RELAYED)][0]
+    return fit(False), fit(True)
 
 
 def rank_program(g, core, T, topo):
     cores = list(T.cores)
     rank = T.rank_of(core)
+    src = sources(cores, topo)
+    half = NP // 2
+
+    def receivers(q):
+        return [None] + [cores[[r for r in range(N) if src[r][s] == q][0]] for s in SLOTS]
 
     def at(c):
         a = topo.addr(c)
         return DstId(rid=a[0], pnc=a[1])
 
-    def send(src, dst, sem, to, engines):
-        a = topo.addr(to)
-        g.remote_dma(dst, src, sem, T.sem.sent, a[1], a[0], bits(engines))
-        return len(engines)
+    def call(*transfers):
+        g.remote_dma_fused([RemoteDMATransfer(dst_ids=[at(c) for c, d in to], dma_engine_mask=bits(e), remote_sem=m,
+                                              srcs=[a], dsts=[d for c, d in to]) for a, e, m, to in transfers],
+                           local_sem=T.sem.sent)
+        return sum(len(e) for a, e, m, to in transfers)
+
+    def u8(buf, a=0, b=NP):
+        return buf[:, a:b].bitcast(dt.uint8)
+
+    group = [[k for k, gr in enumerate(GROUPS) if s in gr][0] for s in range(N)]
+    place = [GROUPS[group[s]].index(s) for s in range(N)]
 
     if rank is None:
         for q, c in enumerate(cores):
             if core not in topo.cores_of(c):
                 continue
-            a, b = relays(c, cores, topo)
-            slots = VIA_A if core == a else VIA_B if core == b else ()
-            full = len(relay_engines(c, core, cores, topo))
-            n = 0
-            for s in slots:
-                to = cores[dest(q, s)]
-                eng = topo.engines(core, to)
-                if s == slots[0]:
-                    g.wait_ge(T.sem.hs, full // 2)
-                n += send(T.hops[:], T["lands%d" % s][:], T.sem["ar%d" % s], to, eng)
-                if s == slots[0]:
-                    g.wait_ge(T.sem.hc, full)
-                n += send(T.hop[:].bitcast(dt.uint8), T["land%d" % s][:].bitcast(dt.uint8), T.sem["ar%d" % s], to, eng)
-            if n:
-                g.wait_ge(T.sem.sent, n)
+            far = receivers(q)
+            a, b = relays(c, far, topo)
+            if core not in (a, b):
+                continue
+            eng = topo.engines(core, far[RELAYED[0]])
+            fed = len([e for e in topo.engines(c, core) if e not in topo.engines(c, far[1])])
+            lo = 0 if core == a else half
+            g.wait_ge(T.sem.hs, fed // 2)
+            planes = RELAYED[0::2] if core == a else RELAYED[1::2]
+            n = call((T.hops[:], eng, T.sem["as%d" % q], [(far[s], T["lands%d" % s][:]) for s in planes]))
+            g.wait_ge(T.sem.hc, fed // 2)
+            for s in RELAYED:
+                n += call((u8(T.hop, lo, lo + half), eng, T.sem["ac%d" % q],
+                           [(far[s], u8(T["land%d" % s], lo, lo + half))]))
+            g.wait_ge(T.sem.sent, n)
         return
 
     V, S, P, Y = g.vector, g.scalar, g.tensor, g.sync
-    relay_a, relay_b = relays(core, cores, topo)
-    far = [None] + [cores[dest(rank, s)] for s in SLOTS]
-    off_eng = topo.engines(core, far[1])
+    far = receivers(rank)
+    relay_a, relay_b = relays(core, far, topo)
+    off = topo.engines(core, far[1])
+    on = [e for e in topo.engines(core, relay_a) if e not in off]
+    eng = len(off)
+    h = eng // 2
 
     Y.dma_start(T.wt[:, 4 * ND:4 * NP], T.wm[:]).then_inc(T.sem.ldw, 16)
+    Y.dma_start(T.wt[:, 0:4 * ND], T.dl[:]).then_inc(T.sem.ldw, 16)
     for t in range(R):
         S.dma_start(T.ixa[0:1, CH * t:CH * t + CH], T.ix[:, 2 * t:2 * t + 2]).then_inc(T.sem.ldi, 16)
-    S.dma_start(T.wt[:, 0:4 * ND], T.dl[:]).then_inc(T.sem.ldw, 16)
-    h = 256 * (R + 1)
-    for i in range(2):
-        S.dma_start(T.xs[:, h * i:h * i + h], T.x[:, h * i:h * i + h]).then_inc(T.sem["xl%d" % i], 16)
+    S.dma_start(T.xs[:], T.x[:]).then_inc(T.sem.ldx, 16)
 
-    g.iota(T.pnum[:], [[0, TC]], 0, 1).then_inc(T.sem.num, 1)
-    g.iota(T.mnum[:], [[16, TC]], 0, 0).then_inc(T.sem.num, 1)
+    def unfold(k, copy, wait):
+        o, f = T["off%d" % k], T["fold%d" % k]
+        w = o.shape[1]
+        for a in range(QD):
+            wait(copy(o[0:32, a:w:QD], f[32 * a:32 * a + 32, :], w // QD), a == QD - 1)
+        wait(copy(o[32:64, :], o[0:32, :], w), True)
+        copy(o[64:128, :], o[0:64, :], w).then_inc(T.sem["of%d" % k], 1)
+
+    g.iota(T.pnum[:], [[0, QM]], 0, 1).then_inc(T.sem.num, 1)
+    g.iota(T.mnum[:], [[16 * QD, QM]], 0, 0).then_inc(T.sem.num, 1)
     g.wait_ge(T.sem.ldi, 16 * R)
     g.partition_broadcast(T.ixr[:], T.ixa[0:1, :], 128).then_inc(T.sem.pb, 1)
 
-    def pools(scale, slots, to):
-        src = T.pools[:] if scale else T.pool[:].bitcast(dt.uint8)
-        tr = []
-        for s in slots:
-            land = T["lands%d" % s][:] if scale else T["land%d" % s][:].bitcast(dt.uint8)
-            tr.append((far[s], topo.engines(core, far[s]), T.sem["ar%d" % s], land))
-        for i, relay in enumerate(to):
-            e = relay_engines(core, relay, cores, topo)
-            w = len(e) // len(to)
-            tr.append((relay, e[w * i:w * i + w], T.sem.hs if scale else T.sem.hc,
-                       T.hops[:] if scale else T.hop[:].bitcast(dt.uint8)))
-        g.remote_dma_fused([RemoteDMATransfer(dst_ids=[at(c)], dma_engine_mask=bits(e), remote_sem=m, srcs=[src], dsts=[d])
-                            for c, e, m, d in tr], local_sem=T.sem.sent)
-        return sum(len(e) for c, e, m, d in tr)
-
-    share = len(off_eng) // (N - 2)
-
-    def lists():
-        tr = []
-        for i, s in enumerate(range(2, N)):
-            e = topo.engines(core, far[s])[share * i:share * i + share]
-            tr.append(RemoteDMATransfer(dst_ids=[at(far[s])], dma_engine_mask=bits(e), remote_sem=T.sem["ls%d" % s],
-                                        srcs=[T.tabd[:]], dsts=[T["lst%d" % s][:]]))
-        g.remote_dma_fused(tr, local_sem=T.sem.sent)
-        return share * (N - 2)
-
+    mine_c, mine_s, mine_l = T.sem["ac%d" % rank], T.sem["as%d" % rank], T.sem["al%d" % rank]
     g.wait_ge(T.sem.qd, 1)
-    sent = pools(True, (1,), (relay_a, relay_b))
-    sent += pools(False, (1,), (relay_a,))
-    g.wait_ge(T.sem.tab, R)
-    sent += send(T.tab[:], T.off1[:], T.sem.ls1, far[1], off_eng)
-    sent += pools(False, (), (relay_b,))
-    g.wait_ge(T.sem.tabd, 16)
-    sent += lists()
+    sent = call((T.pools[:], off, mine_s, [(far[1], T.lands1[:])]),
+                (T.pools[:], on[:h], T.sem.hs, [(relay_a, T.hops[:])]),
+                (T.pools[:], on[h:], T.sem.hs, [(relay_b, T.hops[:])]))
+    sent += call((u8(T.pool, 0, half), off[:h], mine_c, [(far[1], u8(T.land1, 0, half))]),
+                 (u8(T.pool, half, NP), off[h:], mine_c, [(far[1], u8(T.land1, half, NP))]),
+                 (u8(T.pool, 0, half), on[:h], T.sem.hc, [(relay_a, u8(T.hop, 0, half))]),
+                 (u8(T.pool, half, NP), on[h:], T.sem.hc, [(relay_b, u8(T.hop, half, NP))]))
+    g.wait_ge(T.sem.of0, 1)
+    sent += call((T.off0[:], off, mine_l, [(far[1], T.off1[:])]))
+    sent += call((T.fold0[:], off, mine_l,
+                  [(far[s], T["fold%d" % group[s]][:, QC * place[s]:QC * place[s] + QC]) for s in range(2, N)]))
     g.wait_ge(T.sem.sent, sent)
 
     vc = [0]
 
-    def v(ins):
+    def v(ins, last=False):
         vc[0] += 1
         ins.then_inc(T.sem.vc, 1)
+        if last:
+            vwait()
 
     def vwait():
         V.wait_ge(T.sem.vc, vc[0])
@@ -184,61 +197,54 @@ def rank_program(g, core, T, topo):
     v(V.memset(T.stepc[:, CH - 1:ND:CH], 1.0))
     V.wait_ge(T.sem.num, 2)
     v(V.tensor_scalar(T.plow[:], T.pnum[:], 15, None, AluOpType.bitwise_and))
-    vwait()
-    v(V.tensor_tensor(T.ccol[:], T.plow[:], T.mnum[:], AluOpType.add))
-    vwait()
-    v(V.tensor_scalar(T.first[:], T.ccol[:], -1.0, float(-ND), AluOpType.mult, AluOpType.add))
+    v(V.tensor_scalar(T.prun[:], T.pnum[:], 1, 16 * (QD - 1), AluOpType.logical_shift_right, AluOpType.bitwise_and), True)
+    v(V.tensor_tensor(T.cpart[:], T.plow[:], T.prun[:], AluOpType.add), True)
+    v(V.tensor_tensor(T.ccol[:], T.cpart[:], T.mnum[:], AluOpType.add), True)
+    v(V.tensor_scalar(T.first[:], T.ccol[:], -1.0, float(-ND), AluOpType.mult, AluOpType.add), True)
 
     V.wait_ge(T.sem.ldw, 32)
     V.quantize_mx(T.pool[:], T.pools[:], T.wt[:]).then_inc(T.sem.qd, 1)
 
     V.wait_ge(T.sem.pb, 1)
-    v(V.tensor_copy(T.ixb[:], T.ixr[:]))
-    vwait()
-    for m in range(TC):
-        v(V.tensor_scalar(T.ne[:, ND * m:ND * m + ND], T.ixb[:], T.ccol[:, m:m + 1], None, AluOpType.not_equal))
-    vwait()
-    for m in range(TC):
+    for m in range(QM):
+        v(V.tensor_scalar(T.ne[:, ND * m:ND * m + ND], T.ixr[:], T.ccol[:, m:m + 1], None, AluOpType.not_equal), m == QM - 1)
+    for m in range(QM):
         k = slice(ND * m, ND * m + ND)
-        v(V.tensor_tensor_scan(T.stt[:, k], T.ne[:, k], T.stepc[:], T.first[:, m:m + 1], AluOpType.mult, AluOpType.add))
-    vwait()
+        v(V.tensor_tensor_scan(T.stt[:, k], T.ne[:, k], T.stepc[:], T.first[:, m:m + 1], AluOpType.mult, AluOpType.add),
+          m == QM - 1)
     for t in range(1, R + 1):
-        V.tensor_scalar(T.tab[:, TC * (t - 1):TC * t], T.stt[:, CH * t - 1:TC * ND:ND], -1.0, float(CH * t),
-                        AluOpType.mult, AluOpType.add).then_inc(T.sem.tab, 1)
-
-    for i in range(2):
-        V.wait_ge(T.sem["xl%d" % i], 16)
-        k = slice(128 * (R + 1) // 2 * i, 128 * (R + 1) // 2 * (i + 1))
-        V.quantize_mx(T.xq[:, k], T.xqs[:, k], T.xs[:, h * i:h * i + h]).then_inc(T.sem["xq%d" % i], 1)
+        v(V.tensor_scalar(T.fold0[:, QM * (t - 1):QM * t], T.stt[:, CH * t - 1:QM * ND:ND], -1.0, float(CH * t),
+                          AluOpType.mult, AluOpType.add), t == R)
+    unfold(0, lambda o, i, n: V.tensor_copy(o, i), v)
 
     codes = [T.pool] + [T["land%d" % s] for s in SLOTS]
     scales = [T.pools] + [T["lands%d" % s] for s in SLOTS]
-    offs = [T.tab] + [T["off%d" % s] for s in SLOTS]
-    eng = len(off_eng)
 
-    def have(q, s):
+    def have(q, s, kind):
         if s == 0:
             q.wait_ge(T.sem.qd, 1)
+        elif kind == "c":
+            q.wait_ge(T.sem["ac%d" % src[rank][s]], eng if s in DIRECT else 2 * eng)
         else:
-            q.wait_ge(T.sem["ar%d" % s], 2 * eng)
+            q.wait_ge(T.sem["as%d" % src[rank][s]], eng)
 
     def listed(q, s):
-        if s == 0:
-            q.wait_ge(T.sem.tab, R)
-        elif s == 1:
-            q.wait_ge(T.sem.ls1, eng)
+        if s == 1:
+            q.wait_ge(T.sem["al%d" % src[rank][s]], eng)
         else:
-            q.wait_ge(T.sem["rp%d" % s], 64)
+            q.wait_ge(T.sem["of%d" % group[s]], 1)
 
     def column(s, t):
-        return (t * N + source(rank, s)) * SH
+        return (t * N + src[rank][s]) * SH
 
     first_t = {}
 
     def pick(q, s, a, b):
-        have(q, s)
-        listed(q, s)
-        o = offs[s][:, TC * (a - 1):TC * b]
+        if a == 1:
+            have(q, s, "c" if q is V else "s")
+            if place[s] == 0:
+                listed(q, s)
+        o = T["off%d" % group[s]][:, LC * place[s] + TC * (a - 1):LC * place[s] + TC * b]
         k = slice(SH * (a - 1), SH * b)
         for t in range(a, b + 1):
             first_t[(s, t)] = a
@@ -249,10 +255,8 @@ def rank_program(g, core, T, topo):
             S.activation(T["pks%d" % s][:, k], scales[s][:].indirect(o), ActivationFunctionType.Copy
                          ).then_inc(T.sem["ps%d%d" % (s, a)], 1)
 
-    items = [(s, t) for s in range(N - 2) for t in range(R + 1)] + [(s, t) for t in range(R + 1) for s in (N - 2, N - 1)]
-
     def bank(s, t):
-        b = 512 * (items.index((s, t)) % 8)
+        b = 512 * (TENSOR.index((s, t)) % 8)
         return T.acc[:, b:b + SH]
 
     def evac(q, s, t):
@@ -263,61 +267,51 @@ def rank_program(g, core, T, topo):
         else:
             S.activation(T.ys[:, c:c + SH], bank(s, t), ActivationFunctionType.Copy).then_inc(T.sem["ev%d%d" % (s, t)], 1)
 
-    for q, a, b in ((V, 0, 2), (S, 1, 3)):
-        for s in range(N - 2):
-            pick(q, s, 1, 1)
-            if s in (1, 3):
-                evac(q, s - 1, b)
-            if q is V:
-                evac(q, s, a)
-            pick(q, s, 2, 3)
-            if q is S:
-                evac(q, s, a)
-            if s == 1:
-                evac(q, s, b)
-        mine = 4 if q is V else 5
-        pick(q, 4, 1, 1)
-        evac(q, 3, b)
-        pick(q, 5, 1, 1)
-        evac(q, mine, 0)
-        for t in (2, 3):
-            pick(q, 4, t, t)
-            pick(q, 5, t, t)
-            evac(q, mine, t - 1)
-        evac(q, mine, 3)
+    for q, work in ((V, VECTOR), (S, SCALAR)):
+        for w in work:
+            if w[0] == "p":
+                pick(q, int(w[1]), int(w[2]), int(w[3]))
+            elif w[0] == "e":
+                evac(q, int(w[1]), int(w[2]))
+            elif w[0] == "u":
+                for s in RELAYED:
+                    V.wait_ge(T.sem["al%d" % src[rank][s]], eng)
+                unfold(2, lambda o, i, n: V.tensor_copy(o, i), v)
+            else:
+                V.wait_ge(T.sem.ldx, 16)
+                V.quantize_mx(T.xq[:], T.xqs[:], T.xs[:]).then_inc(T.sem.xq, 1)
 
-    for n, (s, t) in enumerate(items):
-        if n == 0:
-            P.wait_ge(T.sem.xq0, 1)
-        if n == 2:
-            P.wait_ge(T.sem.xq1, 1)
+    P.wait_ge(T.sem.xq, 1)
+    for n, (s, t) in enumerate(TENSOR):
         if n >= 8:
-            P.wait_ge(T.sem["ev%d%d" % items[n - 8]], 1)
+            P.wait_ge(T.sem["ev%d%d" % TENSOR[n - 8]], 1)
         if t == 0:
-            have(P, s)
+            have(P, s, "c")
+            if s:
+                have(P, s, "s")
             rhs, rs = codes[s][:, ND:NP], scales[s][:, ND:NP]
         else:
-            a = first_t[(s, t)]
-            if a == t:
-                P.wait_ge(T.sem["pv%d%d" % (s, a)], 1)
-                P.wait_ge(T.sem["ps%d%d" % (s, a)], 1)
+            if first_t[(s, t)] == t:
+                P.wait_ge(T.sem["pv%d%d" % (s, t)], 1)
+                P.wait_ge(T.sem["ps%d%d" % (s, t)], 1)
             k = slice(SH * (t - 1), SH * t)
             rhs, rs = T["pk%d" % s][:, k], T["pks%d" % s][:, k]
         P.matmul_mx(bank(s, t), T.xq[:, 128 * t:128 * t + 128], T.xqs[:, 128 * t:128 * t + 128], rhs, rs, True, True
                     ).then_inc(T.sem["mm%d%d" % (s, t)], 1)
 
-    Y.wait_ge(T.sem.tab, R)
-    Y.dma_start(T.tabd[:], T.tab[0:32, :]).then_inc(T.sem.tabd, 16)
-    for s in range(2, N):
-        Y.wait_ge(T.sem["ls%d" % s], share)
-        for a in range(4):
-            Y.dma_start(T["off%d" % s][32 * a:32 * a + 32, :], T["lst%d" % s][:]).then_inc(T.sem["rp%d" % s], 16)
-    n = 0
+    runs = []
     for s in range(0, N, 2):
-        for t in range(R + 1):
-            c = min(column(s, t), column(s + 1, t))
-            Y.wait_ge(T.sem["ev%d%d" % (s, t)], 1)
-            Y.wait_ge(T.sem["ev%d%d" % (s + 1, t)], 1)
-            Y.dma_start(T.y[:, c:c + 2 * SH], T.ys[:, c:c + 2 * SH]).then_inc(T.sem.st, 16)
-            n += 16
+        for c, b in sorted((column(k, t), (k, t)) for k in (s, s + 1) for t in range(R + 1)):
+            if runs and runs[-1][0] == s and runs[-1][2] == c:
+                runs[-1][2] = c + SH
+                runs[-1][3].append(b)
+            else:
+                runs.append([s, c, c + SH, [b]])
+    runs.sort(key=lambda r: max(TENSOR.index(b) for b in r[3]))
+    n = 0
+    for s, a, b, blocks in runs:
+        for k in blocks:
+            Y.wait_ge(T.sem["ev%d%d" % k], 1)
+        Y.dma_start(T.y[:, a:b], T.ys[:, a:b]).then_inc(T.sem.st, 16)
+        n += 16
     Y.wait_ge(T.sem.st, n)

@@ -3,23 +3,21 @@ from concourse.mybir import dt, AluOpType, ActivationFunctionType
 
 N, SH, CH, R = 6, 192, 32, 3
 ND = R * CH
-NP = ND + SH
+NP = SH + ND
 TC = SH // 16
 LC = R * TC
 QD = 4
 QM = TC // QD
 QC = R * QM
 SLOTS = range(1, N)
-DIRECT, RELAYED = (1,), (2, 3, 4, 5)
-GROUPS = ((0,), DIRECT, RELAYED)
+RELAYED = (2, 3, 4, 5)
+WIDE = ("11", "51")
 
 SCRATCH = {
     "wt": ("sbuf", [128, 4 * NP], "bfloat16"),
     "xs": ("sbuf", [128, 512 * (R + 1)], "bfloat16"),
     "xq": ("sbuf", [128, 128 * (R + 1)], "float8_e4m3fn_x4"),
     "xqs": ("sbuf", [128, 128 * (R + 1)], "uint8"),
-    "pool": ("sbuf", [128, NP], "float8_e4m3fn_x4"),
-    "pools": ("sbuf", [128, NP], "uint8"),
     "hop": ("sbuf", [128, NP], "float8_e4m3fn_x4"),
     "hops": ("sbuf", [128, NP], "uint8"),
     "ixa": ("sbuf", [128, ND], "int32"),
@@ -33,45 +31,45 @@ SCRATCH = {
     "ccol": ("sbuf", [128, QM], "float32"),
     "first": ("sbuf", [128, QM], "float32"),
     "ne": ("sbuf", [128, QM * ND], "bfloat16"),
-    "stt": ("sbuf", [128, QM * ND], "bfloat16"),
+    "stt": ("sbuf", [128, QM * ND], "float32"),
+    "fold0": ("sbuf", [128, QC], "uint16"),
+    "fold2": ("sbuf", [128, 2 * QC], "uint16"),
+    "fold4": ("sbuf", [128, 2 * QC], "uint16"),
+    "off0": ("sbuf", [128, LC], "uint16"),
+    "off1": ("sbuf", [128, LC], "uint16"),
+    "off2": ("sbuf", [128, 2 * LC], "uint16"),
+    "off4": ("sbuf", [128, 2 * LC], "uint16"),
     "ys": ("sbuf", [128, (R + 1) * N * SH], "float32"),
     "acc": ("psum", [128, 8 * 512], "float32"),
 }
-for _k, _g in enumerate(GROUPS):
-    SCRATCH["off%d" % _k] = ("sbuf", [128, LC * len(_g)], "uint16")
-    if _k != 1:
-        SCRATCH["fold%d" % _k] = ("sbuf", [128, QC * len(_g)], "uint16")
 for _s in range(N):
+    SCRATCH["pool%d" % _s] = ("sbuf", [128, NP], "float8_e4m3fn_x4")
+    SCRATCH["plane%d" % _s] = ("sbuf", [128, NP], "uint8")
     SCRATCH["pk%d" % _s] = ("sbuf", [128, R * SH], "float8_e4m3fn_x4")
     SCRATCH["pks%d" % _s] = ("sbuf", [128, R * SH], "uint8")
-for _s in SLOTS:
-    SCRATCH["land%d" % _s] = ("sbuf", [128, NP], "float8_e4m3fn_x4")
-    SCRATCH["lands%d" % _s] = ("sbuf", [128, NP], "uint8")
+for _w in WIDE:
+    SCRATCH["wide" + _w[0]] = ("sbuf", [128, SH + CH], "float32")
 
-SEMAPHORES = (["ldw", "ldi", "ldx", "pb", "num", "vc", "gq", "qd", "xq", "fold", "sent", "st", "hc", "hs"]
-              + ["of%d" % k for k in range(len(GROUPS))]
+TENSOR = "00 01 02 03 10 11 13 12 20 30 21 23 22 33 32 31 40 51 50 41 43 42 52 53".split()
+VECTOR = "f x0 p013 x1 e00 e02 p123 u e12 g1 p213 p313 e21 e23 e22 e32 p411 p423 e51 p522 g5 p533 e42 e43".split()
+SCALAR = "p013 e01 e03 p123 e10 e11 e13 p213 e20 p313 e30 p411 e33 e31 p423 e40 e50 p522 e41 p533 e52 e53".split()
+PICKS = [w[1:] for w in VECTOR if w[0] == "p"]
+
+SEMAPHORES = (["ldw", "ldd", "ldi", "ldx0", "ldx1", "pb", "num", "vc", "qd", "xq0", "xq1", "sent", "st", "hc", "hs",
+               "fold", "gq", "of0", "of2", "of4"] + ["gv" + w[0] for w in WIDE] + ["ne%d" % m for m in range(QM)]
               + ["%s%d" % (k, q) for k in ("ac", "as", "al") for q in range(N)]
-              + ["%s%d%d" % (k, s, t) for k in ("pv", "ps") for s in range(N) for t in (1, 2, 3)]
-              + ["%s%d%d" % (k, s, t) for k in ("mm", "ev") for s in range(N) for t in range(R + 1)])
-
-VECTOR = ("p013 x e02 p113 u e13 p213 p313 e21 e23 p411 e31 p511 e33 p422 e40 p522 e41 p433 p533 e42 e43").split()
-SCALAR = ("p013 e00 e01 e03 e10 p113 e11 e12 p213 e20 p313 e22 e30 p411 e32 p511 p422 e50 p522 e51 p433 p533 e52 e53").split()
-TENSOR = [(s, t) for s in range(N - 2) for t in range(R + 1)] + [(s, t) for t in range(R + 1) for s in (N - 2, N - 1)]
+              + [k + w for k in ("pv", "ps") for w in PICKS]
+              + [k + w for k in ("mm", "ev") for w in TENSOR])
 
 
 def sources(cores, topo):
-    chips = [topo.chip(c) for c in cores]
-    mated = [[q for q in range(N) if q != r and topo.mates(chips[r], chips[q])] for r in range(N)]
-    alone = [r for r in range(N) if not mated[r]]
-    partner = [mated[r][0] if mated[r] else [q for q in alone if q != r][0] for r in range(N)]
     out = []
     for r in range(N):
-        plane = [q for q in range(N) if q == r or topo.same_plane(chips[r], chips[q])]
-        i = plane.index(r)
         row = []
-        for k in range(len(plane)):
-            q = plane[(i + k) % len(plane)]
-            row += [q, partner[q]]
+        for k in range(N // 2):
+            a = 2 * ((r // 2 + k) % (N // 2))
+            near = [q for q in (a, a + 1) if q == r or (k and topo.same_plane(topo.chip(cores[r]), topo.chip(cores[q])))][0]
+            row += [near, 2 * a + 1 - near]
         out.append(row)
     return out
 
@@ -84,12 +82,8 @@ def bits(engines):
 
 
 def relays(core, far, topo):
-    mine = [c for c in topo.cores_of(core) if c != core]
-
-    def fit(same):
-        return [c for c in mine if (topo.die(c) == topo.die(core)) == same
-                and all(topo.may_write(c, far[s]) for s in RELAYED)][0]
-    return fit(False), fit(True)
+    return [[c for c in topo.cores_of(core) if c != core and (topo.die(c) == topo.die(core)) == same
+             and all(topo.may_write(c, far[s]) for s in RELAYED)][0] for same in (False, True)]
 
 
 def rank_program(g, core, T, topo):
@@ -114,27 +108,30 @@ def rank_program(g, core, T, topo):
     def u8(buf, a=0, b=NP):
         return buf[:, a:b].bitcast(dt.uint8)
 
-    group = [[k for k, gr in enumerate(GROUPS) if s in gr][0] for s in range(N)]
-    place = [GROUPS[group[s]].index(s) for s in range(N)]
-
     if rank is None:
         for q, c in enumerate(cores):
             if core not in topo.cores_of(c):
                 continue
             far = receivers(q)
-            a, b = relays(c, far, topo)
-            if core not in (a, b):
+            helpers = relays(c, far, topo)
+            if core not in helpers:
                 continue
+            i = helpers.index(core)
             eng = topo.engines(core, far[RELAYED[0]])
-            fed = len([e for e in topo.engines(c, core) if e not in topo.engines(c, far[1])])
-            lo = 0 if core == a else half
-            g.wait_ge(T.sem.hs, fed // 2)
-            planes = RELAYED[0::2] if core == a else RELAYED[1::2]
-            n = call((T.hops[:], eng, T.sem["as%d" % q], [(far[s], T["lands%d" % s][:]) for s in planes]))
-            g.wait_ge(T.sem.hc, fed // 2)
-            for s in RELAYED:
-                n += call((u8(T.hop, lo, lo + half), eng, T.sem["ac%d" % q],
-                           [(far[s], u8(T["land%d" % s], lo, lo + half))]))
+            lo = half * i
+            w = len(eng) // 2
+
+            def plane(s):
+                return call((T.hops[:], eng, T.sem["as%d" % q], [(far[s], T["plane%d" % s][:])]))
+
+            def codes(s, e):
+                return (u8(T.hop, lo, lo + half), e, T.sem["ac%d" % q], [(far[s], u8(T["pool%d" % s], lo, lo + half))])
+
+            g.wait_ge(T.sem.hs, w)
+            n = plane(RELAYED[i])
+            g.wait_ge(T.sem.hc, w)
+            n += call(codes(RELAYED[0], eng)) + call(codes(RELAYED[1], eng)) + plane(RELAYED[2 + i])
+            n += call(codes(RELAYED[2], eng[:w]), codes(RELAYED[3], eng[w:]))
             g.wait_ge(T.sem.sent, n)
         return
 
@@ -146,19 +143,13 @@ def rank_program(g, core, T, topo):
     eng = len(off)
     h = eng // 2
 
-    Y.dma_start(T.wt[:, 4 * ND:4 * NP], T.wm[:]).then_inc(T.sem.ldw, 16)
-    Y.dma_start(T.wt[:, 0:4 * ND], T.dl[:]).then_inc(T.sem.ldw, 16)
+    Y.dma_start(T.wt[:, 0:4 * SH], T.wm[:]).then_inc(T.sem.ldw, 16)
     for t in range(R):
         S.dma_start(T.ixa[0:1, CH * t:CH * t + CH], T.ix[:, 2 * t:2 * t + 2]).then_inc(T.sem.ldi, 16)
-    S.dma_start(T.xs[:], T.x[:]).then_inc(T.sem.ldx, 16)
-
-    def unfold(k, copy, wait):
-        o, f = T["off%d" % k], T["fold%d" % k]
-        w = o.shape[1]
-        for a in range(QD):
-            wait(copy(o[0:32, a:w:QD], f[32 * a:32 * a + 32, :], w // QD), a == QD - 1)
-        wait(copy(o[32:64, :], o[0:32, :], w), True)
-        copy(o[64:128, :], o[0:64, :], w).then_inc(T.sem["of%d" % k], 1)
+    S.dma_start(T.wt[:, 4 * SH:4 * NP], T.dl[:]).then_inc(T.sem.ldd, 16)
+    xh = 256 * (R + 1)
+    for i in range(2):
+        S.dma_start(T.xs[:, xh * i:xh * i + xh], T.x[:, xh * i:xh * i + xh]).then_inc(T.sem["ldx%d" % i], 16)
 
     g.iota(T.pnum[:], [[0, QM]], 0, 1).then_inc(T.sem.num, 1)
     g.iota(T.mnum[:], [[16 * QD, QM]], 0, 0).then_inc(T.sem.num, 1)
@@ -166,18 +157,41 @@ def rank_program(g, core, T, topo):
     g.partition_broadcast(T.ixr[:], T.ixa[0:1, :], 128).then_inc(T.sem.pb, 1)
 
     mine_c, mine_s, mine_l = T.sem["ac%d" % rank], T.sem["as%d" % rank], T.sem["al%d" % rank]
-    g.wait_ge(T.sem.qd, 1)
-    sent = call((T.pools[:], off, mine_s, [(far[1], T.lands1[:])]),
-                (T.pools[:], on[:h], T.sem.hs, [(relay_a, T.hops[:])]),
-                (T.pools[:], on[h:], T.sem.hs, [(relay_b, T.hops[:])]))
-    sent += call((u8(T.pool, 0, half), off[:h], mine_c, [(far[1], u8(T.land1, 0, half))]),
-                 (u8(T.pool, half, NP), off[h:], mine_c, [(far[1], u8(T.land1, half, NP))]),
-                 (u8(T.pool, 0, half), on[:h], T.sem.hc, [(relay_a, u8(T.hop, 0, half))]),
-                 (u8(T.pool, half, NP), on[h:], T.sem.hc, [(relay_b, u8(T.hop, half, NP))]))
+    g.wait_ge(T.sem.qd, 2)
+    sent = call((T.plane0[:], off, mine_s, [(far[1], T.plane1[:])]),
+                (T.plane0[:], on[:h], T.sem.hs, [(relay_a, T.hops[:])]),
+                (T.plane0[:], on[h:], T.sem.hs, [(relay_b, T.hops[:])]))
+    sent += call((u8(T.pool0, 0, half), off[:h], mine_c, [(far[1], u8(T.pool1, 0, half))]),
+                 (u8(T.pool0, half, NP), off[h:], mine_c, [(far[1], u8(T.pool1, half, NP))]),
+                 (u8(T.pool0, 0, half), on[:h], T.sem.hc, [(relay_a, u8(T.hop, 0, half))]),
+                 (u8(T.pool0, half, NP), on[h:], T.sem.hc, [(relay_b, u8(T.hop, half, NP))]))
     g.wait_ge(T.sem.of0, 1)
     sent += call((T.off0[:], off, mine_l, [(far[1], T.off1[:])]))
     sent += call((T.fold0[:], off, mine_l,
-                  [(far[s], T["fold%d" % group[s]][:, QC * place[s]:QC * place[s] + QC]) for s in range(2, N)]))
+                  [(far[s], T["fold%d" % (s - s % 2)][:, QC * (s % 2):QC * (s % 2) + QC]) for s in RELAYED]))
+
+    def unfold(k, q, copy, step):
+        o, f = T["off%d" % k], T["fold%d" % k]
+        w = o.shape[1]
+        if k == 0:
+            q.wait_ge(T.sem.fold, R)
+        else:
+            for s in (k, k + 1):
+                q.wait_ge(T.sem["al%d" % src[rank][s]], eng)
+        for a in range(QD):
+            step(copy(o[0:32, a:w:QD], f[32 * a:32 * a + 32, :], w // QD), a == QD - 1)
+        step(copy(o[32:64, :], o[0:32, :], w), True)
+        copy(o[64:128, :], o[0:64, :], w).then_inc(T.sem["of%d" % k], 1)
+
+    gq = [0]
+
+    def gstep(ins, last):
+        gq[0] += 1
+        ins.then_inc(T.sem.gq, 1)
+        if last:
+            g.wait_ge(T.sem.gq, gq[0])
+
+    unfold(4, g, lambda o, i, n: g.affine_select(o, i, [[0, n]], AluOpType.is_ge, 0.0, 0, 0), gstep)
     g.wait_ge(T.sem.sent, sent)
 
     vc = [0]
@@ -186,10 +200,7 @@ def rank_program(g, core, T, topo):
         vc[0] += 1
         ins.then_inc(T.sem.vc, 1)
         if last:
-            vwait()
-
-    def vwait():
-        V.wait_ge(T.sem.vc, vc[0])
+            V.wait_ge(T.sem.vc, vc[0])
 
     v(V.memset(T.stepc[:, 0:ND:2], 16.0))
     for t in range(R):
@@ -200,118 +211,129 @@ def rank_program(g, core, T, topo):
     v(V.tensor_scalar(T.prun[:], T.pnum[:], 1, 16 * (QD - 1), AluOpType.logical_shift_right, AluOpType.bitwise_and), True)
     v(V.tensor_tensor(T.cpart[:], T.plow[:], T.prun[:], AluOpType.add), True)
     v(V.tensor_tensor(T.ccol[:], T.cpart[:], T.mnum[:], AluOpType.add), True)
-    v(V.tensor_scalar(T.first[:], T.ccol[:], -1.0, float(-ND), AluOpType.mult, AluOpType.add), True)
+    v(V.tensor_scalar(T.first[:], T.ccol[:], -1.0, float(SH), AluOpType.mult, AluOpType.add), True)
 
-    V.wait_ge(T.sem.ldw, 32)
-    V.quantize_mx(T.pool[:], T.pools[:], T.wt[:]).then_inc(T.sem.qd, 1)
+    cut = NP - 128
+    V.wait_ge(T.sem.ldw, 16)
+    V.quantize_mx(T.pool0[:, 0:cut], T.plane0[:, 0:cut], T.wt[:, 0:4 * cut]).then_inc(T.sem.qd, 1)
+    V.wait_ge(T.sem.ldd, 16)
+    V.quantize_mx(T.pool0[:, cut:NP], T.plane0[:, cut:NP], T.wt[:, 4 * cut:4 * NP]).then_inc(T.sem.qd, 1)
 
     V.wait_ge(T.sem.pb, 1)
     for m in range(QM):
-        v(V.tensor_scalar(T.ne[:, ND * m:ND * m + ND], T.ixr[:], T.ccol[:, m:m + 1], None, AluOpType.not_equal), m == QM - 1)
+        V.tensor_scalar(T.ne[:, ND * m:ND * m + ND], T.ixr[:], T.ccol[:, m:m + 1], None, AluOpType.not_equal
+                        ).then_inc(T.sem["ne%d" % m], 1)
     for m in range(QM):
         k = slice(ND * m, ND * m + ND)
+        V.wait_ge(T.sem["ne%d" % m], 1)
         v(V.tensor_tensor_scan(T.stt[:, k], T.ne[:, k], T.stepc[:], T.first[:, m:m + 1], AluOpType.mult, AluOpType.add),
           m == QM - 1)
     for t in range(1, R + 1):
-        v(V.tensor_scalar(T.fold0[:, QM * (t - 1):QM * t], T.stt[:, CH * t - 1:QM * ND:ND], -1.0, float(CH * t),
-                          AluOpType.mult, AluOpType.add), t == R)
-    unfold(0, lambda o, i, n: V.tensor_copy(o, i), v)
+        V.tensor_scalar(T.fold0[:, QM * (t - 1):QM * t], T.stt[:, CH * t - 1:QM * ND:ND], -1.0, float(SH + CH * t),
+                        AluOpType.mult, AluOpType.add).then_inc(T.sem.fold, 1)
 
-    codes = [T.pool] + [T["land%d" % s] for s in SLOTS]
-    scales = [T.pools] + [T["lands%d" % s] for s in SLOTS]
+    waited = set()
+
+    def need(q, name, n):
+        if (q is V, q is S, q is P, name) not in waited:
+            waited.add((q is V, q is S, q is P, name))
+            q.wait_ge(T.sem[name], n)
 
     def have(q, s, kind):
         if s == 0:
-            q.wait_ge(T.sem.qd, 1)
-        elif kind == "c":
-            q.wait_ge(T.sem["ac%d" % src[rank][s]], eng if s in DIRECT else 2 * eng)
+            need(q, "qd", 2)
         else:
-            q.wait_ge(T.sem["as%d" % src[rank][s]], eng)
+            need(q, "a%s%d" % (kind, src[rank][s]), 2 * eng if kind == "c" and s in RELAYED[:2] else eng)
 
-    def listed(q, s):
+    def offsets(q, s, a, b):
         if s == 1:
-            q.wait_ge(T.sem["al%d" % src[rank][s]], eng)
+            need(q, "al%d" % src[rank][1], eng)
         else:
-            q.wait_ge(T.sem["of%d" % group[s]], 1)
+            need(q, "of%d" % (s - s % 2), 1)
+        o, k = (T["off%d" % s], 0) if s < 2 else (T["off%d" % (s - s % 2)], LC * (s % 2))
+        return o[:, k + TC * (a - 1):k + TC * b]
 
-    def column(s, t):
-        return (t * N + src[rank][s]) * SH
+    def column(w):
+        return (int(w[1]) * N + src[rank][int(w[0])]) * SH
 
-    first_t = {}
-
-    def pick(q, s, a, b):
-        if a == 1:
-            have(q, s, "c" if q is V else "s")
-            if place[s] == 0:
-                listed(q, s)
-        o = T["off%d" % group[s]][:, LC * place[s] + TC * (a - 1):LC * place[s] + TC * b]
-        k = slice(SH * (a - 1), SH * b)
-        for t in range(a, b + 1):
-            first_t[(s, t)] = a
+    def pick(q, w):
+        s, a, b = (int(k) for k in w)
+        have(q, s, "c" if q is V else "s")
+        o, c = offsets(q, s, a, b), slice(SH * (a - 1), SH * b)
         if q is V:
-            V.tensor_copy(T["pk%d" % s][:, k].bitcast(dt.uint32), codes[s][:].bitcast(dt.uint32).indirect(o)
-                          ).then_inc(T.sem["pv%d%d" % (s, a)], 1)
+            V.tensor_copy(T["pk%d" % s][:, c].bitcast(dt.uint32), T["pool%d" % s][:].bitcast(dt.uint32).indirect(o)
+                          ).then_inc(T.sem["pv" + w], 1)
         else:
-            S.activation(T["pks%d" % s][:, k], scales[s][:].indirect(o), ActivationFunctionType.Copy
-                         ).then_inc(T.sem["ps%d%d" % (s, a)], 1)
+            S.activation(T["pks%d" % s][:, c], T["plane%d" % s][:].indirect(o), ActivationFunctionType.Copy
+                         ).then_inc(T.sem["ps" + w], 1)
 
-    def bank(s, t):
-        b = 512 * (TENSOR.index((s, t)) % 8)
-        return T.acc[:, b:b + SH]
+    def width(w):
+        return SH + CH if w in WIDE else SH
 
-    def evac(q, s, t):
-        q.wait_ge(T.sem["mm%d%d" % (s, t)], 1)
-        c = column(s, t)
-        if q is V:
-            V.tensor_copy(T.ys[:, c:c + SH], bank(s, t)).then_inc(T.sem["ev%d%d" % (s, t)], 1)
-        else:
-            S.activation(T.ys[:, c:c + SH], bank(s, t), ActivationFunctionType.Copy).then_inc(T.sem["ev%d%d" % (s, t)], 1)
+    def bank(w):
+        b = 512 * (TENSOR.index(w) % 8)
+        return T.acc[:, b:b + width(w)]
+
+    def copy(q, out, in_):
+        return V.tensor_copy(out, in_) if q is V else S.activation(out, in_, ActivationFunctionType.Copy)
+
+    def evac(q, w):
+        q.wait_ge(T.sem["mm" + w], 1)
+        out = T["wide" + w[0]][:] if w in WIDE else T.ys[:, column(w):column(w) + SH]
+        copy(q, out, bank(w)).then_inc(T.sem["ev" + w], 1)
+
+    def gather(q, k):
+        q.wait_ge(T.sem["ev" + k + "1"], 1)
+        c = column(k + "1")
+        copy(q, T.ys[:, c:c + SH], T["wide" + k][:].indirect(offsets(q, int(k), 1, 1))).then_inc(T.sem["gv" + k], 1)
 
     for q, work in ((V, VECTOR), (S, SCALAR)):
         for w in work:
             if w[0] == "p":
-                pick(q, int(w[1]), int(w[2]), int(w[3]))
+                pick(q, w[1:])
             elif w[0] == "e":
-                evac(q, int(w[1]), int(w[2]))
-            elif w[0] == "u":
-                for s in RELAYED:
-                    V.wait_ge(T.sem["al%d" % src[rank][s]], eng)
-                unfold(2, lambda o, i, n: V.tensor_copy(o, i), v)
+                evac(q, w[1:])
+            elif w[0] == "g":
+                gather(q, w[1])
+            elif w[0] in "fu":
+                unfold(0 if w == "f" else 2, V, lambda o, i, n: V.tensor_copy(o, i), v)
             else:
-                V.wait_ge(T.sem.ldx, 16)
-                V.quantize_mx(T.xq[:], T.xqs[:], T.xs[:]).then_inc(T.sem.xq, 1)
+                i = int(w[1])
+                k = slice(xh // 4 * i, xh // 4 * (i + 1))
+                V.wait_ge(T.sem["ldx%d" % i], 16)
+                V.quantize_mx(T.xq[:, k], T.xqs[:, k], T.xs[:, xh * i:xh * i + xh]).then_inc(T.sem["xq%d" % i], 1)
 
-    P.wait_ge(T.sem.xq, 1)
-    for n, (s, t) in enumerate(TENSOR):
+    for n, w in enumerate(TENSOR):
+        s, t = int(w[0]), int(w[1])
+        need(P, "xq%d" % (t // 2), 1)
         if n >= 8:
-            P.wait_ge(T.sem["ev%d%d" % TENSOR[n - 8]], 1)
-        if t == 0:
+            P.wait_ge(T.sem["ev" + TENSOR[n - 8]], 1)
+        if t == 0 or w in WIDE:
             have(P, s, "c")
-            if s:
-                have(P, s, "s")
-            rhs, rs = codes[s][:, ND:NP], scales[s][:, ND:NP]
+            have(P, s, "s")
+            rhs, rs = T["pool%d" % s][:, 0:width(w)], T["plane%d" % s][:, 0:width(w)]
         else:
-            if first_t[(s, t)] == t:
-                P.wait_ge(T.sem["pv%d%d" % (s, t)], 1)
-                P.wait_ge(T.sem["ps%d%d" % (s, t)], 1)
-            k = slice(SH * (t - 1), SH * t)
-            rhs, rs = T["pk%d" % s][:, k], T["pks%d" % s][:, k]
-        P.matmul_mx(bank(s, t), T.xq[:, 128 * t:128 * t + 128], T.xqs[:, 128 * t:128 * t + 128], rhs, rs, True, True
-                    ).then_inc(T.sem["mm%d%d" % (s, t)], 1)
+            made = [k for k in PICKS if k[0] == w[0] and k[1] <= w[1] <= k[2]][0]
+            need(P, "pv" + made, 1)
+            need(P, "ps" + made, 1)
+            c = slice(SH * (t - 1), SH * t)
+            rhs, rs = T["pk%d" % s][:, c], T["pks%d" % s][:, c]
+        P.matmul_mx(bank(w), T.xq[:, 128 * t:128 * t + 128], T.xqs[:, 128 * t:128 * t + 128], rhs, rs, True, True
+                    ).then_inc(T.sem["mm" + w], 1)
 
     runs = []
     for s in range(0, N, 2):
-        for c, b in sorted((column(k, t), (k, t)) for k in (s, s + 1) for t in range(R + 1)):
+        for c, w in sorted((column(w), w) for w in TENSOR if int(w[0]) in (s, s + 1)):
             if runs and runs[-1][0] == s and runs[-1][2] == c:
                 runs[-1][2] = c + SH
-                runs[-1][3].append(b)
+                runs[-1][3].append(w)
             else:
-                runs.append([s, c, c + SH, [b]])
-    runs.sort(key=lambda r: max(TENSOR.index(b) for b in r[3]))
+                runs.append([s, c, c + SH, [w]])
+    runs.sort(key=lambda r: max(TENSOR.index(w) for w in r[3]))
     n = 0
-    for s, a, b, blocks in runs:
-        for k in blocks:
-            Y.wait_ge(T.sem["ev%d%d" % k], 1)
+    for s, a, b, made in runs:
+        for w in made:
+            Y.wait_ge(T.sem["gv" + w[0] if w in WIDE else "ev" + w], 1)
         Y.dma_start(T.y[:, a:b], T.ys[:, a:b]).then_inc(T.sem.st, 16)
         n += 16
     Y.wait_ge(T.sem.st, n)

from concourse.bass import DstId, RemoteDMATransfer
from concourse.mybir import dt, AluOpType, ActivationFunctionType

N, SH, CH, R = 6, 192, 32, 3
ND = R * CH
NP = SH + ND
TC = SH // 16
LC = R * TC
QD = 4
QM = TC // QD
QC = R * QM
SLOTS = range(1, N)
RELAYED = (2, 3, 4, 5)
WIDE = ("11", "51")

SCRATCH = {
    "wt": ("sbuf", [128, 4 * NP], "bfloat16"),
    "xs": ("sbuf", [128, 512 * (R + 1)], "bfloat16"),
    "xq": ("sbuf", [128, 128 * (R + 1)], "float8_e4m3fn_x4"),
    "xqs": ("sbuf", [128, 128 * (R + 1)], "uint8"),
    "hop": ("sbuf", [128, NP], "float8_e4m3fn_x4"),
    "hops": ("sbuf", [128, NP], "uint8"),
    "ixa": ("sbuf", [128, ND], "int32"),
    "ixr": ("sbuf", [128, ND], "int32"),
    "stepc": ("sbuf", [128, ND], "bfloat16"),
    "pnum": ("sbuf", [128, QM], "int32"),
    "plow": ("sbuf", [128, QM], "int32"),
    "prun": ("sbuf", [128, QM], "int32"),
    "mnum": ("sbuf", [128, QM], "int32"),
    "cpart": ("sbuf", [128, QM], "float32"),
    "ccol": ("sbuf", [128, QM], "float32"),
    "first": ("sbuf", [128, QM], "float32"),
    "ne": ("sbuf", [128, QM * ND], "bfloat16"),
    "stt": ("sbuf", [128, QM * ND], "float32"),
    "fold0": ("sbuf", [128, QC], "uint16"),
    "fold2": ("sbuf", [128, 2 * QC], "uint16"),
    "fold4": ("sbuf", [128, 2 * QC], "uint16"),
    "off0": ("sbuf", [128, LC], "uint16"),
    "off1": ("sbuf", [128, LC], "uint16"),
    "off2": ("sbuf", [128, 2 * LC], "uint16"),
    "off4": ("sbuf", [128, 2 * LC], "uint16"),
    "ys": ("sbuf", [128, (R + 1) * N * SH], "float32"),
    "acc": ("psum", [128, 8 * 512], "float32"),
}
for _s in range(N):
    SCRATCH["pool%d" % _s] = ("sbuf", [128, NP], "float8_e4m3fn_x4")
    SCRATCH["plane%d" % _s] = ("sbuf", [128, NP], "uint8")
    SCRATCH["pk%d" % _s] = ("sbuf", [128, R * SH], "float8_e4m3fn_x4")
    SCRATCH["pks%d" % _s] = ("sbuf", [128, R * SH], "uint8")
for _w in WIDE:
    SCRATCH["wide" + _w[0]] = ("sbuf", [128, SH + CH], "float32")

TENSOR = "00 01 02 03 10 11 13 12 20 30 21 23 22 33 32 31 40 51 50 41 43 42 52 53".split()
VECTOR = "f x0 p013 x1 e00 e02 p123 u e12 g1 p213 p313 e21 e23 e22 e32 p411 p423 e51 p522 g5 p533 e42 e43".split()
SCALAR = "p013 e01 e03 p123 e10 e11 e13 p213 e20 p313 e30 p411 e33 e31 p423 e40 e50 p522 e41 p533 e52 e53".split()
PICKS = [w[1:] for w in VECTOR if w[0] == "p"]

SEMAPHORES = (["ldw", "ldd", "ldi", "ldx0", "ldx1", "pb", "num", "vc", "qd", "xq0", "xq1", "sent", "st", "hc", "hs",
               "fold", "gq", "of0", "of2", "of4"] + ["gv" + w[0] for w in WIDE] + ["ne%d" % m for m in range(QM)]
              + ["%s%d" % (k, q) for k in ("ac", "as", "al") for q in range(N)]
              + [k + w for k in ("pv", "ps") for w in PICKS]
              + [k + w for k in ("mm", "ev") for w in TENSOR])


def sources(cores, topo):
    out = []
    for r in range(N):
        row = []
        for k in range(N // 2):
            a = 2 * ((r // 2 + k) % (N // 2))
            near = [q for q in (a, a + 1) if q == r or (k and topo.same_plane(topo.chip(cores[r]), topo.chip(cores[q])))][0]
            row += [near, 2 * a + 1 - near]
        out.append(row)
    return out


def bits(engines):
    m = 0
    for e in engines:
        m |= 1 << e
    return m


def relays(core, far, topo):
    return [[c for c in topo.cores_of(core) if c != core and (topo.die(c) == topo.die(core)) == same
             and all(topo.may_write(c, far[s]) for s in RELAYED)][0] for same in (False, True)]


def rank_program(g, core, T, topo):
    cores = list(T.cores)
    rank = T.rank_of(core)
    src = sources(cores, topo)
    half = NP // 2

    def receivers(q):
        return [None] + [cores[[r for r in range(N) if src[r][s] == q][0]] for s in SLOTS]

    def at(c):
        a = topo.addr(c)
        return DstId(rid=a[0], pnc=a[1])

    def call(*transfers):
        g.remote_dma_fused([RemoteDMATransfer(dst_ids=[at(c) for c, d in to], dma_engine_mask=bits(e), remote_sem=m,
                                              srcs=[a], dsts=[d for c, d in to]) for a, e, m, to in transfers],
                           local_sem=T.sem.sent)
        return sum(len(e) for a, e, m, to in transfers)

    def u8(buf, a=0, b=NP):
        return buf[:, a:b].bitcast(dt.uint8)

    if rank is None:
        for q, c in enumerate(cores):
            if core not in topo.cores_of(c):
                continue
            far = receivers(q)
            helpers = relays(c, far, topo)
            if core not in helpers:
                continue
            i = helpers.index(core)
            eng = topo.engines(core, far[RELAYED[0]])
            lo = half * i
            w = len(eng) // 2

            def plane(s):
                return call((T.hops[:], eng, T.sem["as%d" % q], [(far[s], T["plane%d" % s][:])]))

            def codes(s, e):
                return (u8(T.hop, lo, lo + half), e, T.sem["ac%d" % q], [(far[s], u8(T["pool%d" % s], lo, lo + half))])

            g.wait_ge(T.sem.hs, w)
            n = plane(RELAYED[i])
            g.wait_ge(T.sem.hc, w)
            n += call(codes(RELAYED[0], eng)) + call(codes(RELAYED[1], eng)) + plane(RELAYED[2 + i])
            n += call(codes(RELAYED[2], eng[:w]), codes(RELAYED[3], eng[w:]))
            g.wait_ge(T.sem.sent, n)
        return

    V, S, P, Y = g.vector, g.scalar, g.tensor, g.sync
    far = receivers(rank)
    relay_a, relay_b = relays(core, far, topo)
    off = topo.engines(core, far[1])
    on = [e for e in topo.engines(core, relay_a) if e not in off]
    eng = len(off)
    h = eng // 2

    Y.dma_start(T.wt[:, 0:4 * SH], T.wm[:]).then_inc(T.sem.ldw, 16)
    for t in range(R):
        S.dma_start(T.ixa[0:1, CH * t:CH * t + CH], T.ix[:, 2 * t:2 * t + 2]).then_inc(T.sem.ldi, 16)
    S.dma_start(T.wt[:, 4 * SH:4 * NP], T.dl[:]).then_inc(T.sem.ldd, 16)
    xh = 256 * (R + 1)
    for i in range(2):
        S.dma_start(T.xs[:, xh * i:xh * i + xh], T.x[:, xh * i:xh * i + xh]).then_inc(T.sem["ldx%d" % i], 16)

    g.iota(T.pnum[:], [[0, QM]], 0, 1).then_inc(T.sem.num, 1)
    g.iota(T.mnum[:], [[16 * QD, QM]], 0, 0).then_inc(T.sem.num, 1)
    g.wait_ge(T.sem.ldi, 16 * R)
    g.partition_broadcast(T.ixr[:], T.ixa[0:1, :], 128).then_inc(T.sem.pb, 1)

    mine_c, mine_s, mine_l = T.sem["ac%d" % rank], T.sem["as%d" % rank], T.sem["al%d" % rank]
    g.wait_ge(T.sem.qd, 2)
    sent = call((T.plane0[:], off, mine_s, [(far[1], T.plane1[:])]),
                (T.plane0[:], on[:h], T.sem.hs, [(relay_a, T.hops[:])]),
                (T.plane0[:], on[h:], T.sem.hs, [(relay_b, T.hops[:])]))
    sent += call((u8(T.pool0, 0, half), off[:h], mine_c, [(far[1], u8(T.pool1, 0, half))]),
                 (u8(T.pool0, half, NP), off[h:], mine_c, [(far[1], u8(T.pool1, half, NP))]),
                 (u8(T.pool0, 0, half), on[:h], T.sem.hc, [(relay_a, u8(T.hop, 0, half))]),
                 (u8(T.pool0, half, NP), on[h:], T.sem.hc, [(relay_b, u8(T.hop, half, NP))]))
    g.wait_ge(T.sem.of0, 1)
    sent += call((T.off0[:], off, mine_l, [(far[1], T.off1[:])]))
    sent += call((T.fold0[:], off, mine_l,
                  [(far[s], T["fold%d" % (s - s % 2)][:, QC * (s % 2):QC * (s % 2) + QC]) for s in RELAYED]))

    def unfold(k, q, copy, step):
        o, f = T["off%d" % k], T["fold%d" % k]
        w = o.shape[1]
        if k == 0:
            q.wait_ge(T.sem.fold, R)
        else:
            for s in (k, k + 1):
                q.wait_ge(T.sem["al%d" % src[rank][s]], eng)
        for a in range(QD):
            step(copy(o[0:32, a:w:QD], f[32 * a:32 * a + 32, :], w // QD), a == QD - 1)
        step(copy(o[32:64, :], o[0:32, :], w), True)
        copy(o[64:128, :], o[0:64, :], w).then_inc(T.sem["of%d" % k], 1)

    gq = [0]

    def gstep(ins, last):
        gq[0] += 1
        ins.then_inc(T.sem.gq, 1)
        if last:
            g.wait_ge(T.sem.gq, gq[0])

    unfold(4, g, lambda o, i, n: g.affine_select(o, i, [[0, n]], AluOpType.is_ge, 0.0, 0, 0), gstep)
    g.wait_ge(T.sem.sent, sent)

    vc = [0]

    def v(ins, last=False):
        vc[0] += 1
        ins.then_inc(T.sem.vc, 1)
        if last:
            V.wait_ge(T.sem.vc, vc[0])

    v(V.memset(T.stepc[:, 0:ND:2], 16.0))
    for t in range(R):
        v(V.memset(T.stepc[:, CH * t + 1:CH * t + CH - 1:2], -15.0))
    v(V.memset(T.stepc[:, CH - 1:ND:CH], 1.0))
    V.wait_ge(T.sem.num, 2)
    v(V.tensor_scalar(T.plow[:], T.pnum[:], 15, None, AluOpType.bitwise_and))
    v(V.tensor_scalar(T.prun[:], T.pnum[:], 1, 16 * (QD - 1), AluOpType.logical_shift_right, AluOpType.bitwise_and), True)
    v(V.tensor_tensor(T.cpart[:], T.plow[:], T.prun[:], AluOpType.add), True)
    v(V.tensor_tensor(T.ccol[:], T.cpart[:], T.mnum[:], AluOpType.add), True)
    v(V.tensor_scalar(T.first[:], T.ccol[:], -1.0, float(SH), AluOpType.mult, AluOpType.add), True)

    cut = NP - 128
    V.wait_ge(T.sem.ldw, 16)
    V.quantize_mx(T.pool0[:, 0:cut], T.plane0[:, 0:cut], T.wt[:, 0:4 * cut]).then_inc(T.sem.qd, 1)
    V.wait_ge(T.sem.ldd, 16)
    V.quantize_mx(T.pool0[:, cut:NP], T.plane0[:, cut:NP], T.wt[:, 4 * cut:4 * NP]).then_inc(T.sem.qd, 1)

    V.wait_ge(T.sem.pb, 1)
    for m in range(QM):
        V.tensor_scalar(T.ne[:, ND * m:ND * m + ND], T.ixr[:], T.ccol[:, m:m + 1], None, AluOpType.not_equal
                        ).then_inc(T.sem["ne%d" % m], 1)
    for m in range(QM):
        k = slice(ND * m, ND * m + ND)
        V.wait_ge(T.sem["ne%d" % m], 1)
        v(V.tensor_tensor_scan(T.stt[:, k], T.ne[:, k], T.stepc[:], T.first[:, m:m + 1], AluOpType.mult, AluOpType.add),
          m == QM - 1)
    for t in range(1, R + 1):
        V.tensor_scalar(T.fold0[:, QM * (t - 1):QM * t], T.stt[:, CH * t - 1:QM * ND:ND], -1.0, float(SH + CH * t),
                        AluOpType.mult, AluOpType.add).then_inc(T.sem.fold, 1)

    waited = set()

    def need(q, name, n):
        if (q is V, q is S, q is P, name) not in waited:
            waited.add((q is V, q is S, q is P, name))
            q.wait_ge(T.sem[name], n)

    def have(q, s, kind):
        if s == 0:
            need(q, "qd", 2)
        else:
            need(q, "a%s%d" % (kind, src[rank][s]), 2 * eng if kind == "c" and s in RELAYED[:2] else eng)

    def offsets(q, s, a, b):
        if s == 1:
            need(q, "al%d" % src[rank][1], eng)
        else:
            need(q, "of%d" % (s - s % 2), 1)
        o, k = (T["off%d" % s], 0) if s < 2 else (T["off%d" % (s - s % 2)], LC * (s % 2))
        return o[:, k + TC * (a - 1):k + TC * b]

    def column(w):
        return (int(w[1]) * N + src[rank][int(w[0])]) * SH

    def pick(q, w):
        s, a, b = (int(k) for k in w)
        have(q, s, "c" if q is V else "s")
        o, c = offsets(q, s, a, b), slice(SH * (a - 1), SH * b)
        if q is V:
            V.tensor_copy(T["pk%d" % s][:, c].bitcast(dt.uint32), T["pool%d" % s][:].bitcast(dt.uint32).indirect(o)
                          ).then_inc(T.sem["pv" + w], 1)
        else:
            S.activation(T["pks%d" % s][:, c], T["plane%d" % s][:].indirect(o), ActivationFunctionType.Copy
                         ).then_inc(T.sem["ps" + w], 1)

    def width(w):
        return SH + CH if w in WIDE else SH

    def bank(w):
        b = 512 * (TENSOR.index(w) % 8)
        return T.acc[:, b:b + width(w)]

    def copy(q, out, in_):
        return V.tensor_copy(out, in_) if q is V else S.activation(out, in_, ActivationFunctionType.Copy)

    def evac(q, w):
        q.wait_ge(T.sem["mm" + w], 1)
        out = T["wide" + w[0]][:] if w in WIDE else T.ys[:, column(w):column(w) + SH]
        copy(q, out, bank(w)).then_inc(T.sem["ev" + w], 1)

    def gather(q, k):
        q.wait_ge(T.sem["ev" + k + "1"], 1)
        c = column(k + "1")
        copy(q, T.ys[:, c:c + SH], T["wide" + k][:].indirect(offsets(q, int(k), 1, 1))).then_inc(T.sem["gv" + k], 1)

    for q, work in ((V, VECTOR), (S, SCALAR)):
        for w in work:
            if w[0] == "p":
                pick(q, w[1:])
            elif w[0] == "e":
                evac(q, w[1:])
            elif w[0] == "g":
                gather(q, w[1])
            elif w[0] in "fu":
                unfold(0 if w == "f" else 2, V, lambda o, i, n: V.tensor_copy(o, i), v)
            else:
                i = int(w[1])
                k = slice(xh // 4 * i, xh // 4 * (i + 1))
                V.wait_ge(T.sem["ldx%d" % i], 16)
                V.quantize_mx(T.xq[:, k], T.xqs[:, k], T.xs[:, xh * i:xh * i + xh]).then_inc(T.sem["xq%d" % i], 1)

    for n, w in enumerate(TENSOR):
        s, t = int(w[0]), int(w[1])
        need(P, "xq%d" % (t // 2), 1)
        if n >= 8:
            P.wait_ge(T.sem["ev" + TENSOR[n - 8]], 1)
        if t == 0 or w in WIDE:
            have(P, s, "c")
            have(P, s, "s")
            rhs, rs = T["pool%d" % s][:, 0:width(w)], T["plane%d" % s][:, 0:width(w)]
        else:
            made = [k for k in PICKS if k[0] == w[0] and k[1] <= w[1] <= k[2]][0]
            need(P, "pv" + made, 1)
            need(P, "ps" + made, 1)
            c = slice(SH * (t - 1), SH * t)
            rhs, rs = T["pk%d" % s][:, c], T["pks%d" % s][:, c]
        P.matmul_mx(bank(w), T.xq[:, 128 * t:128 * t + 128], T.xqs[:, 128 * t:128 * t + 128], rhs, rs, True, True
                    ).then_inc(T.sem["mm" + w], 1)

    runs = []
    for s in range(0, N, 2):
        for c, w in sorted((column(w), w) for w in TENSOR if int(w[0]) in (s, s + 1)):
            if runs and runs[-1][0] == s and runs[-1][2] == c:
                runs[-1][2] = c + SH
                runs[-1][3].append(w)
            else:
                runs.append([s, c, c + SH, [w]])
    runs.sort(key=lambda r: max(TENSOR.index(w) for w in r[3]))
    n = 0
    for s, a, b, made in runs:
        for w in made:
            Y.wait_ge(T.sem["gv" + w[0] if w in WIDE else "ev" + w], 1)
        Y.dma_start(T.y[:, a:b], T.ys[:, a:b]).then_inc(T.sem.st, 16)
        n += 16
    Y.wait_ge(T.sem.st, n)
